import numpy as np
import ml_dtypes


def mxq(x, axis, fmt="e4m3"):
    dtype, down = {"e4m3": (ml_dtypes.float8_e4m3fn, 7), "e5m2": (ml_dtypes.float8_e5m2, 14)}[fmt]
    v = np.moveaxis(np.asarray(x, np.float32).astype(ml_dtypes.bfloat16).astype(np.float64), axis, -1)
    blocks = v.reshape(v.shape[:-1] + (-1, 32))
    amax = np.abs(blocks).max(-1, keepdims=True)
    byte = np.maximum(np.where(amax > 0, np.frexp(amax)[1] - 1 + 127, 0) - down, 1)
    scale = np.exp2(byte - 127.0)
    codes = (blocks / scale).astype(np.float32).astype(dtype).astype(np.float64)
    return np.moveaxis((codes * scale).reshape(v.shape), -1, axis)


WIDE = False


def mx_kscale(k):
    if not WIDE:
        return np.ones(k)
    levels = np.array([30, -30])
    if k % 512:
        return np.exp2(np.random.permutation(np.resize(levels, k // 32))).repeat(32)
    a = np.empty((k // 512, 16))
    for p in range(k // 512):
        a[p, :8] = np.random.permutation(np.resize(levels, 8))
        for g in range(8):
            far = levels[np.abs(levels - a[p, g]) >= 10]
            a[p, g + 8] = far[np.random.randint(len(far))]
    return np.exp2(a.ravel()).repeat(32)


def f64(x):
    return np.asarray(x).astype(np.float64)


def striped(idx):
    return np.tile(idx.reshape(-1, 16).T, (8, 1)).astype(np.uint16)


def unstriped(offs):
    return offs[:16].T.reshape(-1).astype(np.int64)


def d_silu(v):
    s = 1.0 / (1.0 + np.exp(-np.maximum(v, -700.0)))
    return s * (1.0 + v * (1.0 - s))


K, T, E, C, H, N = 128, 2048, 2, 1024, 512, 512


def by_expert(wq, xq):
    return np.concatenate([wq[e].T @ xq[:, e * C:(e + 1) * C] for e in range(E)], axis=1)


def setup_inputs():
    n = np.random.standard_normal
    slot_token = np.random.permutation(T)[:E * C]
    s = mx_kscale(N)[:, None]
    z = np.ones(T); z[slot_token] = mx_kscale(E * C)
    return {
        "xT": (n((K, T)) * z[None, :]).astype(np.float32),
        "dyT": (n((N, T)) * s).astype(np.float32),
        "a": n((H, E * C)).astype(np.float32),
        "w2": (n((E, N, H)) / np.sqrt(N) / s[None]).astype(np.float32),
        "gate": np.tile(np.random.uniform(0.2, 1.0, E * C) / z[slot_token], (N, 1)).astype(np.float32),
        "offs": striped(slot_token),
    }


def reference(xT, dyT, a, w2, gate, offs):
    idx = unstriped(offs)
    gq = mxq(f64(gate) * f64(dyT)[:, idx], 0, "e5m2")
    dh = by_expert(mxq(f64(w2), 1, "e4m3"), gq)
    da = mxq(dh * d_silu(f64(a)), 1, "e5m2")
    xq = mxq(f64(xT)[:, idx], 1, "e4m3")
    return np.stack([(xq[:, e * C:(e + 1) * C] @ da[:, e * C:(e + 1) * C].T) for e in range(E)])

@@ -1,0 +1,266 @@
+from contextlib import ExitStack
+
+import concourse.mybir as mybir
+from concourse.masks import make_identity
+
+K, T, E, C, H, N = 128, 2048, 2, 1024, 512, 512
+FLOPS = 2 * E * C * H * (N + K)
+BYTES = 4 * (K * T + N * T + H * E * C + E * N * H + E * C + E * K * H) + 2 * E * C
+
+F32 = mybir.dt.float32
+BF16 = mybir.dt.bfloat16
+U32 = mybir.dt.uint32
+U16 = mybir.dt.uint16
+U8 = mybir.dt.uint8
+E4M3 = mybir.dt.float8_e4m3fn_x4
+E5M2 = mybir.dt.float8_e5m2_x4
+ACT = mybir.ActivationFunctionType
+MULT = mybir.AluOpType.mult
+SUB = mybir.AluOpType.subtract
+
+P = 128
+PACK = 4
+PASS = P * PACK
+CHUNKS = E * C // PASS
+PER_EXPERT = C // PASS
+BLOCKS = H // P
+RUN = 4
+
+
+def tile_moe_mlp_silu_kernel(tc, xT, dyT, a, w2, gate, offs, out):
+    nc = tc.nc
+    with ExitStack() as ctx:
+        keep = ctx.enter_context(tc.tile_pool(name="keep", bufs=1))
+        ring = ctx.enter_context(tc.tile_pool(name="ring", bufs=2))
+        psum = ctx.enter_context(tc.psum_pool(name="psum", bufs=1))
+
+        offsets = keep.tile([P, E * C // 16], U16, name="offsets")
+        nc.sync.dma_start(offsets[:], offs)
+        ident = keep.tile([P, P], F32, name="ident")
+        make_identity(nc, ident[:])
+
+        dy_rows = dyT.rearrange("(p j) s -> p j s", j=PACK)
+        a_rows = a.rearrange("(b p) s -> p b s", p=P)
+        x_sb = keep.tile([K, T], F32, name="x_sb")
+        gates = keep.tile([P, E * C], F32, name="gates")
+        dy = [keep.tile([P, T], F32, name="dy%d" % t) for t in range(PACK)]
+        pre = [keep.tile([P, BLOCKS * PASS], F32, name="pre%d" % c) for c in range(CHUNKS)]
+        msilu = [keep.tile([P, BLOCKS * PASS], F32, name="msilu%d" % c) for c in range(CHUNKS)]
+        w_raw = [keep.tile([P, PACK * H], F32, name="w_raw%d" % e) for e in range(E)]
+        g32 = [keep.tile([P, PACK * C], F32, name="g32_%d" % e) for e in range(E)]
+        g_mx, w_mx, da_mx, x_mx, acc, da, da_t, x_g = {}, {}, {}, {}, {}, {}, {}, {}
+
+        def listed(first, count):
+            return offsets[:, first // 16 : (first + count) // 16]
+
+        def load_dy(t):
+            nc.sync.dma_start(out=dy[t][:], in_=dy_rows[:, t, :])
+
+        def load_gate(first, count):
+            nc.sync.dma_start(out=gates[:, first : first + count], in_=gate[0:P, first : first + count])
+
+        def load_a(c, first, count):
+            nc.sync.dma_start(
+                out=pre[c][:, first * PASS : (first + count) * PASS].rearrange("p (b s) -> p b s", b=count),
+                in_=a_rows[:, first : first + count, c * PASS : (c + 1) * PASS],
+            )
+
+        def load_w(e):
+            nc.sync.dma_start(out=w_raw[e][:], in_=w2[e].rearrange("(p j) i -> p (j i)", j=PACK))
+
+        def interleave(planes):
+            grouped = ring.tile([P, PASS * PACK], BF16, name="grouped", align_bytes=64)
+            nc.scalar.copy(
+                out=grouped[:].rearrange("p (c r t) -> p c t r", r=RUN, t=PACK),
+                in_=planes.rearrange("p t (c r) -> p c t r", r=RUN),
+            )
+            return grouped[:]
+
+        def w_planes(e):
+            return w_raw[e][:].rearrange("p (t i) -> p t i", t=PACK)
+
+        def g_planes(c):
+            e, half = divmod(c, PER_EXPERT)
+            return g32[e][:].rearrange("p (t s) -> p t s", t=PACK)[:, :, half * PASS : (half + 1) * PASS]
+
+        def mx_tiles(width, name):
+            codes = keep.tile([P, width], U32, name=name + "_codes", align_bytes=64)
+            scales = keep.tile([P, width], U8, name=name + "_scales", align_bytes=64)
+            return codes, scales
+
+        def quantize(values, fmt, tiles, first=0):
+            cols = slice(first, first + values.shape[1] // PACK)
+            nc.vector.quantize_mx(out=tiles[0][:, cols].bitcast(fmt), scales=tiles[1][:, cols], in_=values)
+
+        def activations(c, first, count):
+            cols = slice(first * PASS, (first + count) * PASS)
+            nc.scalar.activation(out=msilu[c][:, cols], in_=pre[c][:, cols], func=ACT.Silu, scale=-1.0)
+            nc.scalar.activation(out=pre[c][:, cols], in_=pre[c][:, cols], func=ACT.Tanh, scale=-0.5)
+
+        def gather_dy(t, first, count):
+            e, at = divmod(first, C)
+            nc.vector.tensor_tensor(
+                g32[e][:, t * C + at : t * C + at + count],
+                dy[t][:].indirect(listed(first, count)),
+                gates[:, first : first + count],
+                MULT,
+            )
+
+        def first_product(c, first, count):
+            e = c // PER_EXPERT
+            for b in range(first, first + count):
+                cols = slice(b * P, (b + 1) * P)
+                dh = psum.tile([P, PASS], F32, name="dh", bufs=4)
+                nc.tensor.matmul_mx(
+                    out=dh[:],
+                    lhsT=w_mx[e][0][:, cols].bitcast(E4M3),
+                    lhsT_scale=w_mx[e][1][:, cols],
+                    rhs=g_mx[c][0][:].bitcast(E5M2),
+                    rhs_scale=g_mx[c][1][:],
+                    start=True,
+                    stop=True,
+                )
+                part = msilu[c][:, b * PASS : (b + 1) * PASS]
+                nc.vector.scalar_tensor_tensor(out=part, in0=part, scalar=1.0, in1=dh[:], op0=SUB, op1=MULT)
+
+        def finish_da(c, first, count):
+            if first == 0:
+                da[c] = ring.tile([P, BLOCKS * PASS], BF16, name="da", align_bytes=64)
+            cols = slice(first * PASS, (first + count) * PASS)
+            nc.vector.scalar_tensor_tensor(
+                out=da[c][:, cols], in0=pre[c][:, cols], scalar=1.0, in1=msilu[c][:, cols], op0=SUB, op1=MULT
+            )
+
+        def turn(rows, turned):
+            count = rows.shape[1] // PASS
+            words = rows.bitcast(F32)
+            bank = psum.tile([P, 2, 2, P], F32, name="turn", bufs=2)
+            for b in range(count):
+                for u in range(2):
+                    nc.tensor.transpose(bank[:, b, u, :], words[:, 2 * P * b + u : 2 * P * (b + 1) : 2], ident[:])
+            nc.scalar.copy(
+                out=turned.rearrange("p (b r u) -> p b r u", b=count, u=2),
+                in_=bank[:, 0:count].rearrange("p b u r -> p b r u"),
+            )
+
+        def turn_da(c, first, count):
+            if first == 0:
+                da_t[c] = ring.tile([P, 2 * H], F32, name="da_t", align_bytes=64)
+            turn(da[c][:, first * PASS : (first + count) * PASS], da_t[c][:, first * 2 * P : (first + count) * 2 * P])
+
+        def quantize_da(c, first, count):
+            if first == 0:
+                da_mx[c] = mx_tiles(H, "da%d" % c)
+            quantize(da_t[c][:, first * 2 * P : (first + count) * 2 * P].bitcast(BF16), E5M2, da_mx[c], first * P)
+
+        def turn_x(e):
+            x_t = ring.tile([P, 4 * K], F32, name="x_t", align_bytes=64)
+            turn(x_g[e][:], x_t[:])
+            return x_t[:].bitcast(BF16)
+
+        def second_product(c):
+            e, half = divmod(c, PER_EXPERT)
+            if half == 0:
+                acc[e] = psum.tile([K, H], F32, name="acc", bufs=2)
+            cols = slice(half * K, (half + 1) * K)
+            nc.tensor.matmul_mx(
+                out=acc[e][:],
+                lhsT=x_mx[e][0][:, cols].bitcast(E4M3),
+                lhsT_scale=x_mx[e][1][:, cols],
+                rhs=da_mx[c][0][:].bitcast(E5M2),
+                rhs_scale=da_mx[c][1][:],
+                start=(half == 0),
+                stop=(half == PER_EXPERT - 1),
+            )
+            if half == PER_EXPERT - 1:
+                result = ring.tile([K, H], F32, name="result")
+                nc.scalar.activation(out=result[:], in_=acc[e][:], func=ACT.Copy, scale=0.5)
+                nc.sync.dma_start(out=out[e], in_=result[:])
+
+        for e in range(E):
+            x_g[e] = ring.tile([P, C], BF16, name="x_g", align_bytes=64)
+            x_mx[e] = mx_tiles(PER_EXPERT * K, "x%d" % e)
+            w_mx[e] = mx_tiles(H, "w%d" % e)
+        for c in range(CHUNKS):
+            g_mx[c] = mx_tiles(PASS, "g%d" % c)
+
+        nc.sync.dma_start(out=x_sb[:], in_=xT)
+        load_gate(0, PASS)
+        load_dy(0)
+        load_gate(PASS, PASS)
+        load_gate(C, C)
+        load_a(0, 0, 2)
+        load_dy(1)
+        load_a(0, 2, 2)
+        load_a(1, 0, 2)
+        load_dy(2)
+        load_a(1, 2, 2)
+        load_w(0)
+        load_dy(3)
+        load_a(2, 0, 4)
+        load_w(1)
+        load_a(3, 0, 4)
+
+        x_bf = keep.tile([K, T], BF16, name="x_bf")
+        nc.vector.tensor_copy(x_g[0][:], x_sb[:].indirect(listed(0, C)))
+        nc.scalar.copy(out=x_bf[:], in_=x_sb[:])
+        nc.scalar.activation(x_g[1][:], x_bf[:].indirect(listed(C, C)), ACT.Copy)
+        gather_dy(0, 0, PASS)
+        gather_dy(0, PASS, PASS)
+        gather_dy(0, C, C)
+        x_in = [turn_x(e) for e in range(E)]
+        for c in range(2):
+            activations(c, 0, 2)
+            activations(c, 2, 2)
+        for t in (1, 2):
+            quantize(x_in[t - 1], E4M3, x_mx[t - 1])
+            for e in range(E):
+                gather_dy(t, e * C, C)
+        w_in = interleave(w_planes(0))
+        gather_dy(3, 0, PASS)
+        g_in = interleave(g_planes(0))
+        quantize(w_in, E4M3, w_mx[0])
+        gather_dy(3, PASS, PASS)
+        gather_dy(3, 2 * PASS, PASS)
+        quantize(g_in, E5M2, g_mx[0])
+        g_in = interleave(g_planes(1))
+        gather_dy(3, 3 * PASS, PASS)
+        first_product(0, 0, 4)
+        quantize(g_in, E5M2, g_mx[1])
+        w_in = interleave(w_planes(1))
+        g_in = interleave(g_planes(2))
+        finish_da(0, 0, 4)
+        turn_da(0, 0, 2)
+        turn_da(0, 2, 2)
+        activations(2, 0, 4)
+        first_product(1, 0, 4)
+        quantize(w_in, E4M3, w_mx[1])
+        quantize(g_in, E5M2, g_mx[2])
+        finish_da(1, 0, 4)
+        quantize_da(0, 0, 4)
+        g_in = interleave(g_planes(3))
+        second_product(0)
+        turn_da(1, 0, 2)
+        turn_da(1, 2, 2)
+        activations(3, 0, 4)
+        first_product(2, 0, 4)
+        quantize(g_in, E5M2, g_mx[3])
+        finish_da(2, 0, 4)
+        quantize_da(1, 0, 4)
+        second_product(1)
+        turn_da(2, 0, 2)
+        turn_da(2, 2, 2)
+        first_product(3, 0, 3)
+        finish_da(3, 0, 2)
+        turn_da(3, 0, 2)
+        first_product(3, 3, 1)
+        finish_da(3, 2, 1)
+        turn_da(3, 2, 1)
+        quantize_da(2, 0, 4)
+        second_product(2)
+        finish_da(3, 3, 1)
+        turn_da(3, 3, 1)
+        quantize_da(3, 0, 2)
+        quantize_da(3, 2, 1)
+        quantize_da(3, 3, 1)
+        second_product(3)

@@ -24,7 +24,11 @@ PASS = P * PACK
 CHUNKS = E * C // PASS
 PER_EXPERT = C // PASS
 BLOCKS = H // P
+STRIPE = 16
 RUN = 4
+PAIR = 2
+STAGED = 3
+ALIGN = 64
 
 
 def tile_moe_mlp_silu_kernel(tc, xT, dyT, a, w2, gate, offs, out):
@@ -34,233 +38,246 @@ def tile_moe_mlp_silu_kernel(tc, xT, dyT, a, w2, gate, offs, out):
         ring = ctx.enter_context(tc.tile_pool(name="ring", bufs=2))
         psum = ctx.enter_context(tc.psum_pool(name="psum", bufs=1))
 
-        offsets = keep.tile([P, E * C // 16], U16, name="offsets")
+        offsets = keep.tile([P, E * C // STRIPE], U16, name="offsets")
         nc.sync.dma_start(offsets[:], offs)
         ident = keep.tile([P, P], F32, name="ident")
         make_identity(nc, ident[:])
 
-        dy_rows = dyT.rearrange("(p j) s -> p j s", j=PACK)
-        a_rows = a.rearrange("(b p) s -> p b s", p=P)
         x_sb = keep.tile([K, T], F32, name="x_sb")
+        x_bf = keep.tile([K, T], BF16, name="x_bf")
+        x_slots = keep.tile([K, E * C], BF16, name="x_slots", align_bytes=ALIGN)
         gates = keep.tile([P, E * C], F32, name="gates")
-        dy = [keep.tile([P, T], F32, name="dy%d" % t) for t in range(PACK)]
-        pre = [keep.tile([P, BLOCKS * PASS], F32, name="pre%d" % c) for c in range(CHUNKS)]
-        msilu = [keep.tile([P, BLOCKS * PASS], F32, name="msilu%d" % c) for c in range(CHUNKS)]
+        dy = [keep.tile([P, T], F32, name="dy%d" % t, align_bytes=ALIGN) for t in range(PACK)]
+        tanhs = [keep.tile([P, BLOCKS * C], F32, name="tanhs%d" % e) for e in range(E)]
+        silus = [keep.tile([P, BLOCKS * C], F32, name="silus%d" % e) for e in range(E)]
         w_raw = [keep.tile([P, PACK * H], F32, name="w_raw%d" % e) for e in range(E)]
-        g32 = [keep.tile([P, PACK * C], F32, name="g32_%d" % e) for e in range(E)]
-        g_mx, w_mx, da_mx, x_mx, acc, da, da_t, x_g = {}, {}, {}, {}, {}, {}, {}, {}
+        g_raw = [keep.tile([P, PACK * C], F32, name="g_raw%d" % e) for e in range(E)]
 
-        def listed(first, count):
-            return offsets[:, first // 16 : (first + count) // 16]
+        def mx_tiles(name):
+            codes = keep.tile([P, PASS], U32, name=name + "_codes", align_bytes=ALIGN)
+            scales = keep.tile([P, PASS], U8, name=name + "_scales", align_bytes=ALIGN)
+            return codes, scales
+
+        w_mx = [mx_tiles("w%d" % e) for e in range(E)]
+        g_mx = [mx_tiles("g%d" % c) for c in range(CHUNKS)]
+        da_rows, da_turned, da_mx, sums = {}, {}, {}, {}
 
         def load_dy(t):
-            nc.sync.dma_start(out=dy[t][:], in_=dy_rows[:, t, :])
+            nc.sync.dma_start(out=dy[t][:], in_=dyT.rearrange("(p t) s -> p t s", t=PACK)[:, t, :])
 
         def load_gate(first, count):
             nc.sync.dma_start(out=gates[:, first : first + count], in_=gate[0:P, first : first + count])
 
-        def load_a(c, first, count):
+        def load_a(e, first, count):
             nc.sync.dma_start(
-                out=pre[c][:, first * PASS : (first + count) * PASS].rearrange("p (b s) -> p b s", b=count),
-                in_=a_rows[:, first : first + count, c * PASS : (c + 1) * PASS],
+                out=tanhs[e][:, first * C : (first + count) * C].rearrange("p (b s) -> p b s", b=count),
+                in_=a.rearrange("(b p) s -> p b s", p=P)[:, first : first + count, e * C : (e + 1) * C],
             )
 
         def load_w(e):
-            nc.sync.dma_start(out=w_raw[e][:], in_=w2[e].rearrange("(p j) i -> p (j i)", j=PACK))
+            nc.sync.dma_start(out=w_raw[e][:], in_=w2[e].rearrange("(p t) i -> p (t i)", t=PACK))
 
-        def interleave(planes):
-            grouped = ring.tile([P, PASS * PACK], BF16, name="grouped", align_bytes=64)
-            nc.scalar.copy(
-                out=grouped[:].rearrange("p (c r t) -> p c t r", r=RUN, t=PACK),
-                in_=planes.rearrange("p t (c r) -> p c t r", r=RUN),
-            )
-            return grouped[:]
+        def listed(first, count):
+            return offsets[:, first // STRIPE : (first + count) // STRIPE]
 
-        def w_planes(e):
-            return w_raw[e][:].rearrange("p (t i) -> p t i", t=PACK)
-
-        def g_planes(c):
-            e, half = divmod(c, PER_EXPERT)
-            return g32[e][:].rearrange("p (t s) -> p t s", t=PACK)[:, :, half * PASS : (half + 1) * PASS]
-
-        def mx_tiles(width, name):
-            codes = keep.tile([P, width], U32, name=name + "_codes", align_bytes=64)
-            scales = keep.tile([P, width], U8, name=name + "_scales", align_bytes=64)
-            return codes, scales
-
-        def quantize(values, fmt, tiles, first=0):
-            cols = slice(first, first + values.shape[1] // PACK)
-            nc.vector.quantize_mx(out=tiles[0][:, cols].bitcast(fmt), scales=tiles[1][:, cols], in_=values)
-
-        def activations(c, first, count):
-            cols = slice(first * PASS, (first + count) * PASS)
-            nc.scalar.activation(out=msilu[c][:, cols], in_=pre[c][:, cols], func=ACT.Silu, scale=-1.0)
-            nc.scalar.activation(out=pre[c][:, cols], in_=pre[c][:, cols], func=ACT.Tanh, scale=-0.5)
-
-        def gather_dy(t, first, count):
+        def gather_g(t, first, count):
             e, at = divmod(first, C)
             nc.vector.tensor_tensor(
-                g32[e][:, t * C + at : t * C + at + count],
+                g_raw[e][:, t * C + at : t * C + at + count],
                 dy[t][:].indirect(listed(first, count)),
                 gates[:, first : first + count],
                 MULT,
             )
 
+        def interleave(planes):
+            staged = ring.tile([P, PASS * PACK], BF16, name="staged", bufs=STAGED, align_bytes=ALIGN)
+            nc.scalar.copy(
+                out=staged[:].rearrange("p (c r t) -> p c t r", r=RUN, t=PACK),
+                in_=planes.rearrange("p t (c r) -> p c t r", r=RUN),
+            )
+            return staged[:]
+
+        def interleave_w(e):
+            return interleave(w_raw[e][:].rearrange("p (t i) -> p t i", t=PACK))
+
+        def interleave_g(c):
+            e, half = divmod(c, PER_EXPERT)
+            planes = g_raw[e][:].rearrange("p (t s) -> p t s", t=PACK)
+            return interleave(planes[:, :, half * PASS : (half + 1) * PASS])
+
+        def quantize(values, fmt, mx, first=0):
+            cols = slice(first, first + values.shape[1] // PACK)
+            nc.vector.quantize_mx(out=mx[0][:, cols].bitcast(fmt), scales=mx[1][:, cols], in_=values)
+
+        def part(tiles, c, first, count):
+            e, half = divmod(c, PER_EXPERT)
+            blocks = tiles[e][:].rearrange("p (b s) -> p b s", b=BLOCKS)
+            return blocks[:, first : first + count, half * PASS : (half + 1) * PASS]
+
+        def activate(values, silu_out):
+            nc.scalar.activation(out=silu_out, in_=values, func=ACT.Silu, scale=-1.0)
+            nc.scalar.activation(out=values, in_=values, func=ACT.Tanh, scale=-0.5)
+
+        def activate_block(e, b):
+            activate(tanhs[e][:, b * C : (b + 1) * C], silus[e][:, b * C : (b + 1) * C])
+
+        def activate_chunk(c):
+            activate(part(tanhs, c, 0, BLOCKS), part(silus, c, 0, BLOCKS))
+
         def first_product(c, first, count):
-            e = c // PER_EXPERT
+            w_codes, w_scales = w_mx[c // PER_EXPERT]
             for b in range(first, first + count):
                 cols = slice(b * P, (b + 1) * P)
-                dh = psum.tile([P, PASS], F32, name="dh", bufs=4)
+                dh = psum.tile([P, PASS], F32, name="dh", bufs=BLOCKS)
                 nc.tensor.matmul_mx(
                     out=dh[:],
-                    lhsT=w_mx[e][0][:, cols].bitcast(E4M3),
-                    lhsT_scale=w_mx[e][1][:, cols],
+                    lhsT=w_codes[:, cols].bitcast(E4M3),
+                    lhsT_scale=w_scales[:, cols],
                     rhs=g_mx[c][0][:].bitcast(E5M2),
                     rhs_scale=g_mx[c][1][:],
                     start=True,
                     stop=True,
                 )
-                part = msilu[c][:, b * PASS : (b + 1) * PASS]
-                nc.vector.scalar_tensor_tensor(out=part, in0=part, scalar=1.0, in1=dh[:], op0=SUB, op1=MULT)
+                held = part(silus, c, b, 1)[:, 0, :]
+                nc.vector.scalar_tensor_tensor(out=held, in0=held, scalar=1.0, in1=dh[:], op0=SUB, op1=MULT)
 
         def finish_da(c, first, count):
             if first == 0:
-                da[c] = ring.tile([P, BLOCKS * PASS], BF16, name="da", align_bytes=64)
-            cols = slice(first * PASS, (first + count) * PASS)
+                da_rows[c] = ring.tile([P, BLOCKS * PASS], BF16, name="da_rows", align_bytes=ALIGN)
             nc.vector.scalar_tensor_tensor(
-                out=da[c][:, cols], in0=pre[c][:, cols], scalar=1.0, in1=msilu[c][:, cols], op0=SUB, op1=MULT
+                out=da_rows[c][:, first * PASS : (first + count) * PASS].rearrange("p (b s) -> p b s", b=count),
+                in0=part(tanhs, c, first, count),
+                scalar=1.0,
+                in1=part(silus, c, first, count),
+                op0=SUB,
+                op1=MULT,
             )
 
         def turn(rows, turned):
-            count = rows.shape[1] // PASS
+            pieces = rows.shape[1] // PASS
             words = rows.bitcast(F32)
-            bank = psum.tile([P, 2, 2, P], F32, name="turn", bufs=2)
-            for b in range(count):
-                for u in range(2):
-                    nc.tensor.transpose(bank[:, b, u, :], words[:, 2 * P * b + u : 2 * P * (b + 1) : 2], ident[:])
+            bank = psum.tile([P, PAIR, PAIR, P], F32, name="turn", bufs=3)
+            for j in range(pieces):
+                for u in range(PAIR):
+                    every_second = words[:, PAIR * P * j + u : PAIR * P * (j + 1) : PAIR]
+                    nc.tensor.transpose(bank[:, j, u, :], every_second, ident[:])
             nc.scalar.copy(
-                out=turned.rearrange("p (b r u) -> p b r u", b=count, u=2),
-                in_=bank[:, 0:count].rearrange("p b u r -> p b r u"),
+                out=turned.rearrange("p (j r u) -> p j r u", j=pieces, u=PAIR),
+                in_=bank[:, 0:pieces].rearrange("p j u r -> p j r u"),
             )
+
+        def turned_da(c, first, count):
+            return da_turned[c][:, first * PAIR * P : (first + count) * PAIR * P]
 
         def turn_da(c, first, count):
             if first == 0:
-                da_t[c] = ring.tile([P, 2 * H], F32, name="da_t", align_bytes=64)
-            turn(da[c][:, first * PASS : (first + count) * PASS], da_t[c][:, first * 2 * P : (first + count) * 2 * P])
+                da_turned[c] = ring.tile([P, PAIR * H], F32, name="da_turned", align_bytes=ALIGN)
+            turn(da_rows[c][:, first * PASS : (first + count) * PASS], turned_da(c, first, count))
 
         def quantize_da(c, first, count):
             if first == 0:
-                da_mx[c] = mx_tiles(H, "da%d" % c)
-            quantize(da_t[c][:, first * 2 * P : (first + count) * 2 * P].bitcast(BF16), E5M2, da_mx[c], first * P)
-
-        def turn_x(e):
-            x_t = ring.tile([P, 4 * K], F32, name="x_t", align_bytes=64)
-            turn(x_g[e][:], x_t[:])
-            return x_t[:].bitcast(BF16)
+                da_mx[c] = mx_tiles("da%d" % c)
+            quantize(turned_da(c, first, count).bitcast(BF16), E5M2, da_mx[c], first * P)
 
         def second_product(c):
             e, half = divmod(c, PER_EXPERT)
             if half == 0:
-                acc[e] = psum.tile([K, H], F32, name="acc", bufs=2)
-            cols = slice(half * K, (half + 1) * K)
+                sums[e] = psum.tile([K, H], F32, name="sums")
+            cols = slice(c * K, (c + 1) * K)
             nc.tensor.matmul_mx(
-                out=acc[e][:],
-                lhsT=x_mx[e][0][:, cols].bitcast(E4M3),
-                lhsT_scale=x_mx[e][1][:, cols],
+                out=sums[e][:],
+                lhsT=x_codes[:, cols].bitcast(E4M3),
+                lhsT_scale=x_scales[:, cols],
                 rhs=da_mx[c][0][:].bitcast(E5M2),
                 rhs_scale=da_mx[c][1][:],
                 start=(half == 0),
                 stop=(half == PER_EXPERT - 1),
             )
-            if half == PER_EXPERT - 1:
-                result = ring.tile([K, H], F32, name="result")
-                nc.scalar.activation(out=result[:], in_=acc[e][:], func=ACT.Copy, scale=0.5)
-                nc.sync.dma_start(out=out[e], in_=result[:])
 
-        for e in range(E):
-            x_g[e] = ring.tile([P, C], BF16, name="x_g", align_bytes=64)
-            x_mx[e] = mx_tiles(PER_EXPERT * K, "x%d" % e)
-            w_mx[e] = mx_tiles(H, "w%d" % e)
-        for c in range(CHUNKS):
-            g_mx[c] = mx_tiles(PASS, "g%d" % c)
+        def store(e):
+            result = ring.tile([K, H], F32, name="result")
+            for first in range(0, H, H // 2):
+                cols = slice(first, first + H // 2)
+                nc.scalar.activation(out=result[:, cols], in_=sums[e][:, cols], func=ACT.Copy, scale=0.5)
+                nc.sync.dma_start(out=out[e][:, cols], in_=result[:, cols])
 
         nc.sync.dma_start(out=x_sb[:], in_=xT)
         load_gate(0, PASS)
         load_dy(0)
         load_gate(PASS, PASS)
         load_gate(C, C)
-        load_a(0, 0, 2)
+        load_a(0, 0, 1)
         load_dy(1)
-        load_a(0, 2, 2)
-        load_a(1, 0, 2)
+        load_a(0, 1, 1)
+        load_a(0, 2, 1)
         load_dy(2)
-        load_a(1, 2, 2)
         load_w(0)
+        load_a(0, 3, 1)
         load_dy(3)
-        load_a(2, 0, 4)
         load_w(1)
-        load_a(3, 0, 4)
+        load_a(1, 0, 2)
+        load_a(1, 2, 2)
 
-        x_bf = keep.tile([K, T], BF16, name="x_bf")
-        nc.vector.tensor_copy(x_g[0][:], x_sb[:].indirect(listed(0, C)))
+        nc.vector.tensor_copy(x_slots[:, 0:C], x_sb[:].indirect(listed(0, C)))
         nc.scalar.copy(out=x_bf[:], in_=x_sb[:])
-        nc.scalar.activation(x_g[1][:], x_bf[:].indirect(listed(C, C)), ACT.Copy)
-        gather_dy(0, 0, PASS)
-        gather_dy(0, PASS, PASS)
-        gather_dy(0, C, C)
-        x_in = [turn_x(e) for e in range(E)]
-        for c in range(2):
-            activations(c, 0, 2)
-            activations(c, 2, 2)
+        nc.scalar.activation(x_slots[:, C : 2 * C], x_bf[:].indirect(listed(C, C)), ACT.Copy)
+
+        gather_g(0, 0, PASS)
+        gather_g(0, PASS, PASS)
+        gather_g(0, C, C)
+        activate_block(0, 0)
+        x_turned = keep.tile([P, CHUNKS * K * PAIR], F32, name="x_turned", tag="dy0", align_bytes=ALIGN)
+        for e in range(E):
+            turn(x_slots[:, e * C : (e + 1) * C], x_turned[:, e * PASS : (e + 1) * PASS])
+        activate_block(0, 1)
+        activate_block(0, 2)
         for t in (1, 2):
-            quantize(x_in[t - 1], E4M3, x_mx[t - 1])
             for e in range(E):
-                gather_dy(t, e * C, C)
-        w_in = interleave(w_planes(0))
-        gather_dy(3, 0, PASS)
-        g_in = interleave(g_planes(0))
-        quantize(w_in, E4M3, w_mx[0])
-        gather_dy(3, PASS, PASS)
-        gather_dy(3, 2 * PASS, PASS)
-        quantize(g_in, E5M2, g_mx[0])
-        g_in = interleave(g_planes(1))
-        gather_dy(3, 3 * PASS, PASS)
-        first_product(0, 0, 4)
-        quantize(g_in, E5M2, g_mx[1])
-        w_in = interleave(w_planes(1))
-        g_in = interleave(g_planes(2))
-        finish_da(0, 0, 4)
-        turn_da(0, 0, 2)
-        turn_da(0, 2, 2)
-        activations(2, 0, 4)
-        first_product(1, 0, 4)
-        quantize(w_in, E4M3, w_mx[1])
-        quantize(g_in, E5M2, g_mx[2])
-        finish_da(1, 0, 4)
-        quantize_da(0, 0, 4)
-        g_in = interleave(g_planes(3))
-        second_product(0)
-        turn_da(1, 0, 2)
-        turn_da(1, 2, 2)
-        activations(3, 0, 4)
-        first_product(2, 0, 4)
-        quantize(g_in, E5M2, g_mx[3])
-        finish_da(2, 0, 4)
-        quantize_da(1, 0, 4)
-        second_product(1)
-        turn_da(2, 0, 2)
-        turn_da(2, 2, 2)
-        first_product(3, 0, 3)
-        finish_da(3, 0, 2)
-        turn_da(3, 0, 2)
-        first_product(3, 3, 1)
-        finish_da(3, 2, 1)
-        turn_da(3, 2, 1)
-        quantize_da(2, 0, 4)
-        second_product(2)
-        finish_da(3, 3, 1)
-        turn_da(3, 3, 1)
-        quantize_da(3, 0, 2)
-        quantize_da(3, 2, 1)
-        quantize_da(3, 3, 1)
-        second_product(3)
+                gather_g(t, e * C, C)
+
+        w_staged = interleave_w(0)
+        gather_g(3, 0, PASS)
+        g_staged = {0: interleave_g(0)}
+        gather_g(3, PASS, PASS)
+        activate_block(0, 3)
+        g_staged[1] = interleave_g(1)
+        quantize(w_staged, E4M3, w_mx[0])
+        gather_g(3, 2 * PASS, PASS)
+        quantize(g_staged[0], E5M2, g_mx[0])
+        gather_g(3, 3 * PASS, PASS)
+        w_staged = interleave_w(1)
+        x_codes = ring.tile([P, CHUNKS * K], U32, name="x_codes", tag="staged", bufs=STAGED, align_bytes=ALIGN)
+        x_scales = keep.tile([P, CHUNKS * K], U8, name="x_scales", align_bytes=ALIGN)
+        quantize(x_turned[:].bitcast(BF16), E4M3, (x_codes, x_scales))
+
+        last = CHUNKS - 1
+        for c in range(last):
+            first_product(c, 0, BLOCKS)
+            if c + 1 == PER_EXPERT:
+                quantize(w_staged, E4M3, w_mx[1])
+            quantize(g_staged[c + 1], E5M2, g_mx[c + 1])
+            finish_da(c, 0, BLOCKS)
+            if c + 2 <= last:
+                g_staged[c + 2] = interleave_g(c + 2)
+                activate_chunk(c + 2)
+            if c > 0:
+                quantize_da(c - 1, 0, BLOCKS)
+                second_product(c - 1)
+            for first in range(0, BLOCKS, PAIR):
+                turn_da(c, first, PAIR)
+        store(0)
+
+        pieces = ((0, PAIR), (PAIR, 1), (PAIR + 1, 1))
+        first_product(last, 0, BLOCKS - 1)
+        finish_da(last, *pieces[0])
+        turn_da(last, *pieces[0])
+        first_product(last, BLOCKS - 1, 1)
+        for piece in pieces[1:]:
+            finish_da(last, *piece)
+            turn_da(last, *piece)
+        quantize_da(last - 1, 0, BLOCKS)
+        second_product(last - 1)
+        for piece in pieces:
+            quantize_da(last, *piece)
+        second_product(last)
+        store(1)

@@ -27,7 +27,6 @@ BLOCKS = H // P
 STRIPE = 16
 RUN = 4
 PAIR = 2
-STAGED = 3
 ALIGN = 64
 
 
@@ -89,8 +88,8 @@ def tile_moe_mlp_silu_kernel(tc, xT, dyT, a, w2, gate, offs, out):
                 MULT,
             )
 
-        def interleave(planes):
-            staged = ring.tile([P, PASS * PACK], BF16, name="staged", bufs=STAGED, align_bytes=ALIGN)
+        def interleave(planes, pool):
+            staged = pool.tile([P, PASS * PACK], BF16, name="staged", align_bytes=ALIGN)
             nc.scalar.copy(
                 out=staged[:].rearrange("p (c r t) -> p c t r", r=RUN, t=PACK),
                 in_=planes.rearrange("p t (c r) -> p c t r", r=RUN),
@@ -98,12 +97,12 @@ def tile_moe_mlp_silu_kernel(tc, xT, dyT, a, w2, gate, offs, out):
             return staged[:]
 
         def interleave_w(e):
-            return interleave(w_raw[e][:].rearrange("p (t i) -> p t i", t=PACK))
+            return interleave(w_raw[e][:].rearrange("p (t i) -> p t i", t=PACK), ring)
 
-        def interleave_g(c):
+        def interleave_g(c, pool):
             e, half = divmod(c, PER_EXPERT)
             planes = g_raw[e][:].rearrange("p (t s) -> p t s", t=PACK)
-            return interleave(planes[:, :, half * PASS : (half + 1) * PASS])
+            return interleave(planes[:, :, half * PASS : (half + 1) * PASS], pool)
 
         def quantize(values, fmt, mx, first=0):
             cols = slice(first, first + values.shape[1] // PACK)
@@ -237,16 +236,16 @@ def tile_moe_mlp_silu_kernel(tc, xT, dyT, a, w2, gate, offs, out):
 
         w_staged = interleave_w(0)
         gather_g(3, 0, PASS)
-        g_staged = {0: interleave_g(0)}
+        g_staged = {0: interleave_g(0, keep)}
         gather_g(3, PASS, PASS)
         activate_block(0, 3)
-        g_staged[1] = interleave_g(1)
+        g_staged[1] = interleave_g(1, ring)
         quantize(w_staged, E4M3, w_mx[0])
         gather_g(3, 2 * PASS, PASS)
         quantize(g_staged[0], E5M2, g_mx[0])
         gather_g(3, 3 * PASS, PASS)
         w_staged = interleave_w(1)
-        x_codes = ring.tile([P, CHUNKS * K], U32, name="x_codes", tag="staged", bufs=STAGED, align_bytes=ALIGN)
+        x_codes = keep.tile([P, CHUNKS * K], U32, name="x_codes", tag="staged", align_bytes=ALIGN)
         x_scales = keep.tile([P, CHUNKS * K], U8, name="x_scales", align_bytes=ALIGN)
         quantize(x_turned[:].bitcast(BF16), E4M3, (x_codes, x_scales))
 
@@ -258,7 +257,7 @@ def tile_moe_mlp_silu_kernel(tc, xT, dyT, a, w2, gate, offs, out):
             quantize(g_staged[c + 1], E5M2, g_mx[c + 1])
             finish_da(c, 0, BLOCKS)
             if c + 2 <= last:
-                g_staged[c + 2] = interleave_g(c + 2)
+                g_staged[c + 2] = interleave_g(c + 2, ring)
                 activate_chunk(c + 2)
             if c > 0:
                 quantize_da(c - 1, 0, BLOCKS)

@@ -91,8 +91,8 @@ def tile_moe_mlp_silu_kernel(tc, xT, dyT, a, w2, gate, offs, out):
         def interleave(planes, pool):
             staged = pool.tile([P, PASS * PACK], BF16, name="staged", align_bytes=ALIGN)
             nc.scalar.copy(
-                out=staged[:].rearrange("p (c r t) -> p c t r", r=RUN, t=PACK),
-                in_=planes.rearrange("p t (c r) -> p c t r", r=RUN),
+                out=staged[:].rearrange("p (c r u v) -> p c u r v", r=RUN, u=PAIR, v=PAIR),
+                in_=planes.rearrange("p (u v) (c r) -> p c u r v", r=RUN, v=PAIR),
             )
             return staged[:]
 
@@ -150,6 +150,23 @@ def tile_moe_mlp_silu_kernel(tc, xT, dyT, a, w2, gate, offs, out):
                 in1=part(silus, c, first, count),
                 op0=SUB,
                 op1=MULT,
+            )
+
+        def finish_and_turn_block(c, b):
+            bank = psum.tile([P, PAIR, PAIR, P], F32, name="turn", bufs=3)
+            for u in range(PAIR):
+                half = da_rows[c][:, b * PASS + u * PAIR * P : b * PASS + (u + 1) * PAIR * P]
+                nc.vector.scalar_tensor_tensor(
+                    out=half.rearrange("p (q v) -> p q v", v=PAIR),
+                    in0=part(tanhs, c, b, 1)[:, 0, :].rearrange("p (q u v) -> p u q v", u=PAIR, v=PAIR)[:, u],
+                    scalar=1.0,
+                    in1=part(silus, c, b, 1)[:, 0, :].rearrange("p (q u v) -> p u q v", u=PAIR, v=PAIR)[:, u],
+                    op0=SUB,
+                    op1=MULT,
+                )
+                nc.tensor.transpose(bank[:, 0, u, :], half.bitcast(F32), ident[:])
+            nc.scalar.copy(
+                out=turned_da(c, b, 1).rearrange("p (r u) -> p r u", u=PAIR), in_=bank[:, 0].rearrange("p u r -> p r u")
             )
 
         def turn(rows, turned):
@@ -271,9 +288,8 @@ def tile_moe_mlp_silu_kernel(tc, xT, dyT, a, w2, gate, offs, out):
         finish_da(last, *pieces[0])
         turn_da(last, *pieces[0])
         first_product(last, BLOCKS - 1, 1)
-        for piece in pieces[1:]:
-            finish_da(last, *piece)
-            turn_da(last, *piece)
+        for b in range(PAIR, BLOCKS):
+            finish_and_turn_block(last, b)
         quantize_da(last - 1, 0, BLOCKS)
         second_product(last - 1)
         for piece in pieces:

from contextlib import ExitStack

import concourse.mybir as mybir
from concourse.masks import make_identity

K, T, E, C, H, N = 128, 2048, 2, 1024, 512, 512
FLOPS = 2 * E * C * H * (N + K)
BYTES = 4 * (K * T + N * T + H * E * C + E * N * H + E * C + E * K * H) + 2 * E * C

F32 = mybir.dt.float32
BF16 = mybir.dt.bfloat16
U32 = mybir.dt.uint32
U16 = mybir.dt.uint16
U8 = mybir.dt.uint8
E4M3 = mybir.dt.float8_e4m3fn_x4
E5M2 = mybir.dt.float8_e5m2_x4
ACT = mybir.ActivationFunctionType
MULT = mybir.AluOpType.mult
SUB = mybir.AluOpType.subtract

P = 128
PACK = 4
PASS = P * PACK
CHUNKS = E * C // PASS
PER_EXPERT = C // PASS
BLOCKS = H // P
STRIPE = 16
RUN = 4
PAIR = 2
ALIGN = 64


def tile_moe_mlp_silu_kernel(tc, xT, dyT, a, w2, gate, offs, out):
    nc = tc.nc
    with ExitStack() as ctx:
        keep = ctx.enter_context(tc.tile_pool(name="keep", bufs=1))
        ring = ctx.enter_context(tc.tile_pool(name="ring", bufs=2))
        psum = ctx.enter_context(tc.psum_pool(name="psum", bufs=1))

        offsets = keep.tile([P, E * C // STRIPE], U16, name="offsets")
        nc.sync.dma_start(offsets[:], offs)
        ident = keep.tile([P, P], F32, name="ident")
        make_identity(nc, ident[:])

        x_sb = keep.tile([K, T], F32, name="x_sb")
        x_bf = keep.tile([K, T], BF16, name="x_bf")
        x_slots = keep.tile([K, E * C], BF16, name="x_slots", align_bytes=ALIGN)
        gates = keep.tile([P, E * C], F32, name="gates")
        dy = [keep.tile([P, T], F32, name="dy%d" % t, align_bytes=ALIGN) for t in range(PACK)]
        tanhs = [keep.tile([P, BLOCKS * C], F32, name="tanhs%d" % e) for e in range(E)]
        silus = [keep.tile([P, BLOCKS * C], F32, name="silus%d" % e) for e in range(E)]
        w_raw = [keep.tile([P, PACK * H], F32, name="w_raw%d" % e) for e in range(E)]
        g_raw = [keep.tile([P, PACK * C], F32, name="g_raw%d" % e) for e in range(E)]

        def mx_tiles(name):
            codes = keep.tile([P, PASS], U32, name=name + "_codes", align_bytes=ALIGN)
            scales = keep.tile([P, PASS], U8, name=name + "_scales", align_bytes=ALIGN)
            return codes, scales

        w_mx = [mx_tiles("w%d" % e) for e in range(E)]
        g_mx = [mx_tiles("g%d" % c) for c in range(CHUNKS)]
        da_rows, da_turned, da_mx, sums = {}, {}, {}, {}

        def load_dy(t):
            nc.sync.dma_start(out=dy[t][:], in_=dyT.rearrange("(p t) s -> p t s", t=PACK)[:, t, :])

        def load_gate(first, count):
            nc.sync.dma_start(out=gates[:, first : first + count], in_=gate[0:P, first : first + count])

        def load_a(e, first, count):
            nc.sync.dma_start(
                out=tanhs[e][:, first * C : (first + count) * C].rearrange("p (b s) -> p b s", b=count),
                in_=a.rearrange("(b p) s -> p b s", p=P)[:, first : first + count, e * C : (e + 1) * C],
            )

        def load_w(e):
            nc.sync.dma_start(out=w_raw[e][:], in_=w2[e].rearrange("(p t) i -> p (t i)", t=PACK))

        def listed(first, count):
            return offsets[:, first // STRIPE : (first + count) // STRIPE]

        def gather_g(t, first, count):
            e, at = divmod(first, C)
            nc.vector.tensor_tensor(
                g_raw[e][:, t * C + at : t * C + at + count],
                dy[t][:].indirect(listed(first, count)),
                gates[:, first : first + count],
                MULT,
            )

        def interleave(planes, pool):
            staged = pool.tile([P, PASS * PACK], BF16, name="staged", align_bytes=ALIGN)
            nc.scalar.copy(
                out=staged[:].rearrange("p (c r u v) -> p c u r v", r=RUN, u=PAIR, v=PAIR),
                in_=planes.rearrange("p (u v) (c r) -> p c u r v", r=RUN, v=PAIR),
            )
            return staged[:]

        def interleave_w(e):
            return interleave(w_raw[e][:].rearrange("p (t i) -> p t i", t=PACK), ring)

        def interleave_g(c, pool):
            e, half = divmod(c, PER_EXPERT)
            planes = g_raw[e][:].rearrange("p (t s) -> p t s", t=PACK)
            return interleave(planes[:, :, half * PASS : (half + 1) * PASS], pool)

        def quantize(values, fmt, mx, first=0):
            cols = slice(first, first + values.shape[1] // PACK)
            nc.vector.quantize_mx(out=mx[0][:, cols].bitcast(fmt), scales=mx[1][:, cols], in_=values)

        def part(tiles, c, first, count):
            e, half = divmod(c, PER_EXPERT)
            blocks = tiles[e][:].rearrange("p (b s) -> p b s", b=BLOCKS)
            return blocks[:, first : first + count, half * PASS : (half + 1) * PASS]

        def activate(values, silu_out):
            nc.scalar.activation(out=silu_out, in_=values, func=ACT.Silu, scale=-1.0)
            nc.scalar.activation(out=values, in_=values, func=ACT.Tanh, scale=-0.5)

        def activate_block(e, b):
            activate(tanhs[e][:, b * C : (b + 1) * C], silus[e][:, b * C : (b + 1) * C])

        def activate_chunk(c):
            activate(part(tanhs, c, 0, BLOCKS), part(silus, c, 0, BLOCKS))

        def first_product(c, first, count):
            w_codes, w_scales = w_mx[c // PER_EXPERT]
            for b in range(first, first + count):
                cols = slice(b * P, (b + 1) * P)
                dh = psum.tile([P, PASS], F32, name="dh", bufs=BLOCKS)
                nc.tensor.matmul_mx(
                    out=dh[:],
                    lhsT=w_codes[:, cols].bitcast(E4M3),
                    lhsT_scale=w_scales[:, cols],
                    rhs=g_mx[c][0][:].bitcast(E5M2),
                    rhs_scale=g_mx[c][1][:],
                    start=True,
                    stop=True,
                )
                held = part(silus, c, b, 1)[:, 0, :]
                nc.vector.scalar_tensor_tensor(out=held, in0=held, scalar=1.0, in1=dh[:], op0=SUB, op1=MULT)

        def finish_da(c, first, count):
            if first == 0:
                da_rows[c] = ring.tile([P, BLOCKS * PASS], BF16, name="da_rows", align_bytes=ALIGN)
            nc.vector.scalar_tensor_tensor(
                out=da_rows[c][:, first * PASS : (first + count) * PASS].rearrange("p (b s) -> p b s", b=count),
                in0=part(tanhs, c, first, count),
                scalar=1.0,
                in1=part(silus, c, first, count),
                op0=SUB,
                op1=MULT,
            )

        def finish_and_turn_block(c, b):
            bank = psum.tile([P, PAIR, PAIR, P], F32, name="turn", bufs=3)
            for u in range(PAIR):
                half = da_rows[c][:, b * PASS + u * PAIR * P : b * PASS + (u + 1) * PAIR * P]
                nc.vector.scalar_tensor_tensor(
                    out=half.rearrange("p (q v) -> p q v", v=PAIR),
                    in0=part(tanhs, c, b, 1)[:, 0, :].rearrange("p (q u v) -> p u q v", u=PAIR, v=PAIR)[:, u],
                    scalar=1.0,
                    in1=part(silus, c, b, 1)[:, 0, :].rearrange("p (q u v) -> p u q v", u=PAIR, v=PAIR)[:, u],
                    op0=SUB,
                    op1=MULT,
                )
                nc.tensor.transpose(bank[:, 0, u, :], half.bitcast(F32), ident[:])
            nc.scalar.copy(
                out=turned_da(c, b, 1).rearrange("p (r u) -> p r u", u=PAIR), in_=bank[:, 0].rearrange("p u r -> p r u")
            )

        def turn(rows, turned):
            pieces = rows.shape[1] // PASS
            words = rows.bitcast(F32)
            bank = psum.tile([P, PAIR, PAIR, P], F32, name="turn", bufs=3)
            for j in range(pieces):
                for u in range(PAIR):
                    every_second = words[:, PAIR * P * j + u : PAIR * P * (j + 1) : PAIR]
                    nc.tensor.transpose(bank[:, j, u, :], every_second, ident[:])
            nc.scalar.copy(
                out=turned.rearrange("p (j r u) -> p j r u", j=pieces, u=PAIR),
                in_=bank[:, 0:pieces].rearrange("p j u r -> p j r u"),
            )

        def turned_da(c, first, count):
            return da_turned[c][:, first * PAIR * P : (first + count) * PAIR * P]

        def turn_da(c, first, count):
            if first == 0:
                da_turned[c] = ring.tile([P, PAIR * H], F32, name="da_turned", align_bytes=ALIGN)
            turn(da_rows[c][:, first * PASS : (first + count) * PASS], turned_da(c, first, count))

        def quantize_da(c, first, count):
            if first == 0:
                da_mx[c] = mx_tiles("da%d" % c)
            quantize(turned_da(c, first, count).bitcast(BF16), E5M2, da_mx[c], first * P)

        def second_product(c):
            e, half = divmod(c, PER_EXPERT)
            if half == 0:
                sums[e] = psum.tile([K, H], F32, name="sums")
            cols = slice(c * K, (c + 1) * K)
            nc.tensor.matmul_mx(
                out=sums[e][:],
                lhsT=x_codes[:, cols].bitcast(E4M3),
                lhsT_scale=x_scales[:, cols],
                rhs=da_mx[c][0][:].bitcast(E5M2),
                rhs_scale=da_mx[c][1][:],
                start=(half == 0),
                stop=(half == PER_EXPERT - 1),
            )

        def store(e):
            result = ring.tile([K, H], F32, name="result")
            for first in range(0, H, H // 2):
                cols = slice(first, first + H // 2)
                nc.scalar.activation(out=result[:, cols], in_=sums[e][:, cols], func=ACT.Copy, scale=0.5)
                nc.sync.dma_start(out=out[e][:, cols], in_=result[:, cols])

        nc.sync.dma_start(out=x_sb[:], in_=xT)
        load_gate(0, PASS)
        load_dy(0)
        load_gate(PASS, PASS)
        load_gate(C, C)
        load_a(0, 0, 1)
        load_dy(1)
        load_a(0, 1, 1)
        load_a(0, 2, 1)
        load_dy(2)
        load_w(0)
        load_a(0, 3, 1)
        load_dy(3)
        load_w(1)
        load_a(1, 0, 2)
        load_a(1, 2, 2)

        nc.vector.tensor_copy(x_slots[:, 0:C], x_sb[:].indirect(listed(0, C)))
        nc.scalar.copy(out=x_bf[:], in_=x_sb[:])
        nc.scalar.activation(x_slots[:, C : 2 * C], x_bf[:].indirect(listed(C, C)), ACT.Copy)

        gather_g(0, 0, PASS)
        gather_g(0, PASS, PASS)
        gather_g(0, C, C)
        activate_block(0, 0)
        x_turned = keep.tile([P, CHUNKS * K * PAIR], F32, name="x_turned", tag="dy0", align_bytes=ALIGN)
        for e in range(E):
            turn(x_slots[:, e * C : (e + 1) * C], x_turned[:, e * PASS : (e + 1) * PASS])
        activate_block(0, 1)
        activate_block(0, 2)
        for t in (1, 2):
            for e in range(E):
                gather_g(t, e * C, C)

        w_staged = interleave_w(0)
        gather_g(3, 0, PASS)
        g_staged = {0: interleave_g(0, keep)}
        gather_g(3, PASS, PASS)
        activate_block(0, 3)
        g_staged[1] = interleave_g(1, ring)
        quantize(w_staged, E4M3, w_mx[0])
        gather_g(3, 2 * PASS, PASS)
        quantize(g_staged[0], E5M2, g_mx[0])
        gather_g(3, 3 * PASS, PASS)
        w_staged = interleave_w(1)
        x_codes = keep.tile([P, CHUNKS * K], U32, name="x_codes", tag="staged", align_bytes=ALIGN)
        x_scales = keep.tile([P, CHUNKS * K], U8, name="x_scales", align_bytes=ALIGN)
        quantize(x_turned[:].bitcast(BF16), E4M3, (x_codes, x_scales))

        last = CHUNKS - 1
        for c in range(last):
            first_product(c, 0, BLOCKS)
            if c + 1 == PER_EXPERT:
                quantize(w_staged, E4M3, w_mx[1])
            quantize(g_staged[c + 1], E5M2, g_mx[c + 1])
            finish_da(c, 0, BLOCKS)
            if c + 2 <= last:
                g_staged[c + 2] = interleave_g(c + 2, ring)
                activate_chunk(c + 2)
            if c > 0:
                quantize_da(c - 1, 0, BLOCKS)
                second_product(c - 1)
            for first in range(0, BLOCKS, PAIR):
                turn_da(c, first, PAIR)
        store(0)

        pieces = ((0, PAIR), (PAIR, 1), (PAIR + 1, 1))
        first_product(last, 0, BLOCKS - 1)
        finish_da(last, *pieces[0])
        turn_da(last, *pieces[0])
        first_product(last, BLOCKS - 1, 1)
        for b in range(PAIR, BLOCKS):
            finish_and_turn_block(last, b)
        quantize_da(last - 1, 0, BLOCKS)
        second_product(last - 1)
        for piece in pieces:
            quantize_da(last, *piece)
        second_product(last)
        store(1)
